import numpy as np
import ml_dtypes


def mxq(x, axis, fmt="e4m3"):
    dtype, down = {"e4m3": (ml_dtypes.float8_e4m3fn, 7), "e5m2": (ml_dtypes.float8_e5m2, 14)}[fmt]
    v = np.moveaxis(np.asarray(x, np.float32).astype(ml_dtypes.bfloat16).astype(np.float64), axis, -1)
    blocks = v.reshape(v.shape[:-1] + (-1, 32))
    amax = np.abs(blocks).max(-1, keepdims=True)
    byte = np.maximum(np.where(amax > 0, np.frexp(amax)[1] - 1 + 127, 0) - down, 1)
    scale = np.exp2(byte - 127.0)
    codes = (blocks / scale).astype(np.float32).astype(dtype).astype(np.float64)
    return np.moveaxis((codes * scale).reshape(v.shape), -1, axis)


WIDE = False


def mx_kscale(k):
    if not WIDE:
        return np.ones(k)
    levels = np.array([10, -10, 5, -5, 0])
    if k % 512:
        return np.exp2(np.random.permutation(np.resize(levels, k // 32))).repeat(32)
    a = np.empty((k // 512, 16))
    for p in range(k // 512):
        a[p, :8] = np.random.permutation(np.resize(levels, 8))
        for g in range(8):
            far = levels[np.abs(levels - a[p, g]) >= 10]
            a[p, g + 8] = far[np.random.randint(len(far))]
    return np.exp2(a.ravel()).repeat(32)


def f64(x):
    return np.asarray(x).astype(np.float64)


def striped8(idx):
    return np.asarray(idx).reshape(8, -1, 16).transpose(0, 2, 1).reshape(128, -1).astype(np.uint16)


def unstriped8(offs):
    return offs.reshape(8, 16, -1).transpose(0, 2, 1).reshape(8, -1).astype(np.int64)


def pick8(x, idx, run):
    r = np.arange(len(x))
    return x[r[:, None], idx[r % (8 * run) // run]]


E2M1 = np.array([0.0, 0.5, 1.0, 1.5, 2.0, 3.0, 4.0, 6.0, -0.0, -0.5, -1.0, -1.5, -2.0, -3.0, -4.0, -6.0])


def pack_weight(w, fmt):
    k, n = w.shape
    w = f64(np.asarray(w, np.float32).astype(ml_dtypes.bfloat16)).reshape(k // 32, 32, n)
    amax = np.abs(w).max(1)
    if fmt == "e4m3":
        byte = np.frexp(amax)[1] - 1 + 127 - 7
    else:
        mant, ex = np.frexp(amax / 6.0)
        byte = np.where(mant > 0.5, ex, ex - 1) + 127
    byte = np.clip(np.where(amax > 0, byte, 1), 1, 254)
    scaled = (w * np.exp2(127.0 - byte)[:, None, :]).reshape(k, n).astype(np.float32)
    by_word = np.ascontiguousarray(scaled.reshape(k // 512, 128, 4, n).transpose(0, 1, 3, 2))
    if fmt == "e4m3":
        words = by_word.astype(ml_dtypes.float8_e4m3fn).view(np.uint8)
    else:
        c = by_word.astype(ml_dtypes.float4_e2m1fn).view(np.uint8) & 0xF
        words = (c[..., 0::2] | (c[..., 1::2] << 4)).reshape(k // 512, 128, 2 * n)
    return np.ascontiguousarray(words), np.ascontiguousarray(byte.astype(np.uint8).reshape(k // 512, 16, n))


def unpack_weight(words, scales, fmt):
    g, _, n = scales.shape
    words = np.ascontiguousarray(words).reshape(g, 128, n, -1)
    if fmt == "e4m3":
        vals = words.view(ml_dtypes.float8_e4m3fn).astype(np.float64)
    else:
        nib = np.empty((g, 128, n, 4), np.uint8)
        nib[..., 0::2] = words & 0xF
        nib[..., 1::2] = words >> 4
        vals = E2M1[nib]
    vals = vals * np.repeat(np.exp2(scales.astype(np.float64) - 127.0), 8, axis=1)[..., None]
    return vals.transpose(0, 1, 3, 2).reshape(g * 512, n)


D, T, U, Z, I, Q = 512, 1024, 1024, 1024, 512, 128


def setup_inputs():
    n = np.random.standard_normal
    idx = np.stack([np.random.permutation(T)[:I] for _ in range(8)])
    idx2 = np.stack([np.random.permutation(U)[:I] for _ in range(8)])
    idx3 = np.stack([np.random.permutation(Z)[:I] for _ in range(8)])
    idx4 = np.stack([np.random.permutation(Z)[:I] for _ in range(8)])
    idx5 = np.stack([np.random.permutation(T)[:I] for _ in range(8)])
    fd = mx_kscale(D)
    keysp = pack_weight(n((D, T)) / fd[:, None], "e2m1")
    notesp = pack_weight(n((D, U)) / fd[:, None], "e4m3")
    return {
        "query": (n((D, Q)) * 1.0 / np.sqrt(D) * fd[:, None]).astype(np.float32),
        "keys_words": keysp[0],
        "keys_scales": keysp[1],
        "notes_words": notesp[0],
        "notes_scales": notesp[1],
        "offs": striped8(idx),
        "offs2": striped8(idx2),
        "offs3": striped8(idx3),
        "offs4": striped8(idx4),
        "offs5": striped8(idx5),
    }


def reference(query, keys_words, keys_scales, notes_words, notes_scales, offs, offs2, offs3, offs4, offs5):
    idx = unstriped8(offs)
    idx2 = unstriped8(offs2)
    idx3 = unstriped8(offs3)
    idx4 = unstriped8(offs4)
    idx5 = unstriped8(offs5)
    keysu = unpack_weight(keys_words, keys_scales, "e2m1")
    notesu = unpack_weight(notes_words, notes_scales, "e4m3")
    queryq = mxq(f64(query), 0, "e4m3")
    a = queryq.T @ keysu
    b = queryq.T @ notesu
    f1 = np.zeros((Q, Z))
    f1[np.arange(Q)[:, None], idx3[np.arange(Q) % 128 // 16]] = pick8(a, idx, 16)
    f2 = np.zeros((Q, Z))
    f2[np.arange(Q)[:, None], idx4[np.arange(Q) % 128 // 16]] = pick8(b, idx2, 16)
    m1 = np.maximum(f1, f2)
    w = pick8(m1, idx4, 16) - pick8(m1, idx3, 16)
    f3 = np.zeros((Q, T))
    f3[np.arange(Q)[:, None], idx5[np.arange(Q) % 128 // 16]] = w
    aa = a + f3
    y = pick8(aa, idx, 16)
    return y

@@ -1,0 +1,134 @@
+import concourse.mybir as mybir
+
+F32 = mybir.dt.float32
+BF16 = mybir.dt.bfloat16
+I32 = mybir.dt.int32
+U32 = mybir.dt.uint32
+U16 = mybir.dt.uint16
+U8 = mybir.dt.uint8
+FP8X4 = mybir.dt.float8_e4m3fn_x4
+FP4X4 = mybir.dt.float4_e2m1fn_x4
+ALU = mybir.AluOpType
+COPY = mybir.ActivationFunctionType.Copy
+
+P = 128
+PACK = 4
+D, T, I, Q = 512, 1024, 512, 128
+HALF = I // 2
+LIST_COLS = I // 16
+FLOPS = 2 * 2 * D * Q * T
+
+
+def tile_attend_meetinghall_two_kernel(tc, query, keys_words, keys_scales, notes_words, notes_scales,
+                                        offs, offs2, offs3, offs4, offs5, out):
+    nc = tc.nc
+    with (
+        tc.tile_pool(name="lists", bufs=1) as lists,
+        tc.tile_pool(name="sb", bufs=1) as sb,
+        tc.psum_pool(name="ps", bufs=1) as ps,
+    ):
+        def load_list(name, src):
+            tile = lists.tile([P, LIST_COLS], U16, name=name)
+            nc.sync.dma_start(tile[:], src)
+            return tile
+
+        def half(tile, h):
+            return tile[:, h * LIST_COLS // 2 : (h + 1) * LIST_COLS // 2]
+
+        def load_scales(plane, src):
+            rows = src[0].bitcast(I32)
+            for quad in range(4):
+                nc.sync.dma_start(plane[32 * quad : 32 * quad + 4, :].bitcast(I32), rows[4 * quad : 4 * quad + 4, :])
+
+        key_plane = sb.tile([P, T], U8, name="key_plane", align_bytes=64)
+        note_plane = sb.tile([P, T], U8, name="note_plane", align_bytes=64)
+        nc.vector.memset(key_plane[:].bitcast(I32), 0)
+        nc.vector.memset(note_plane[:].bitcast(I32), 0)
+
+        q_raw = sb.tile([P, PACK, Q], F32, name="q_raw")
+        nc.sync.dma_start(q_raw[:], query.rearrange("(p j) q -> p j q", j=PACK))
+        key_words = sb.tile([P, 2 * T], U8, name="key_words", align_bytes=64)
+        nc.sync.dma_start(key_words[:].bitcast(I32), keys_words[0].bitcast(I32))
+        load_scales(key_plane, keys_scales)
+        idx = load_list("idx", offs)
+        idx3 = load_list("idx3", offs3)
+        note_words = sb.tile([P, T], U32, name="note_words", align_bytes=64)
+        nc.sync.dma_start(note_words[:].bitcast(I32), notes_words[0].rearrange("p n t -> p (n t)").bitcast(I32))
+        load_scales(note_plane, notes_scales)
+        idx2 = load_list("idx2", offs2)
+        idx4 = load_list("idx4", offs4)
+        idx5 = load_list("idx5", offs5)
+
+        f1 = sb.tile([P, T], F32, name="f1")
+        f2 = sb.tile([P, T], F32, name="f2")
+        nc.vector.memset(f1[:].bitcast(I32), 0)
+        nc.vector.memset(f2[:].bitcast(I32), 0)
+
+        q_bf = sb.tile([P, Q * PACK], BF16, name="q_bf", tag="q_bf_then_f3", align_bytes=64)
+        nc.vector.tensor_copy(
+            q_bf[:].rearrange("p (c i t) -> p c t i", i=4, t=PACK),
+            q_raw[:].rearrange("p t (c i) -> p c t i", i=4),
+        )
+        q_codes = sb.tile([P, Q], U32, name="q_codes", align_bytes=64)
+        q_plane = sb.tile([P, Q], U8, name="q_plane", align_bytes=64)
+        nc.vector.quantize_mx(out=q_codes[:].bitcast(FP8X4), scales=q_plane[:], in_=q_bf[:])
+
+        f3 = sb.tile([P, T], F32, name="f3", tag="q_bf_then_f3", align_bytes=64)
+        nc.vector.memset(f3[:].bitcast(I32), 0)
+
+        a = sb.tile([P, T], F32, name="a")
+        for piece in range(4):
+            cols = slice(piece * 256, (piece + 1) * 256)
+            bank = ps.tile([P, 512], F32, name=f"a_bank{piece}", tag=f"bank{piece}")
+            nc.tensor.matmul_mx(
+                out=bank[:, 0:256],
+                lhsT=q_codes[:].bitcast(FP8X4), lhsT_scale=q_plane[:],
+                rhs=key_words[:, 2 * cols.start : 2 * cols.stop].bitcast(FP4X4), rhs_scale=key_plane[:, cols],
+                start=True, stop=True,
+            )
+            if piece % 2 == 0:
+                nc.scalar.activation(a[:, cols], bank[:, 0:256], COPY)
+            else:
+                nc.vector.tensor_copy(a[:, cols], bank[:, 0:256])
+
+        a_picked = [sb.tile([P, HALF], F32, name=f"a_picked{h}") for h in range(2)]
+        nc.scalar.activation(a_picked[0][:], a[:].indirect(half(idx, 0)), COPY)
+        nc.vector.tensor_copy(a_picked[1][:], a[:].indirect(half(idx, 1)))
+        for h in range(2):
+            nc.vector.tensor_copy(f1[:].indirect(half(idx3, h)), a_picked[h][:])
+
+        b = sb.tile([P, T], F32, name="b")
+        for piece in range(2):
+            cols = slice(piece * 512, (piece + 1) * 512)
+            bank = ps.tile([P, 512], F32, name=f"b_bank{piece}", tag=f"bank{2 + piece}")
+            nc.tensor.matmul_mx(
+                out=bank[:],
+                lhsT=q_codes[:].bitcast(FP8X4), lhsT_scale=q_plane[:],
+                rhs=note_words[:, cols].bitcast(FP8X4), rhs_scale=note_plane[:, cols],
+                start=True, stop=True,
+            )
+            nc.scalar.activation(b[:, cols], bank[:], COPY)
+        b_picked = sb.tile([P, I], F32, name="b_picked")
+        nc.scalar.activation(b_picked[:], b[:].indirect(idx2[:]), COPY)
+        nc.vector.tensor_copy(f2[:].indirect(idx4[:]), b_picked[:])
+
+        m1 = sb.tile([P, T], F32, name="m1")
+        nc.vector.tensor_tensor(m1[:], f1[:], f2[:], ALU.max)
+
+        at4 = [sb.tile([P, HALF], F32, name=f"at4_{h}") for h in range(2)]
+        minus_at3 = [sb.tile([P, HALF], F32, name=f"minus_at3_{h}") for h in range(2)]
+        nc.scalar.activation(at4[0][:], m1[:].indirect(half(idx4, 0)), COPY)
+        nc.vector.tensor_scalar(minus_at3[0][:], m1[:].indirect(half(idx3, 0)), -1.0, 0.0, ALU.mult, ALU.add)
+        nc.scalar.activation(at4[1][:], m1[:].indirect(half(idx4, 1)), COPY)
+        nc.scalar.activation(minus_at3[1][:], m1[:].indirect(half(idx3, 1)), COPY, scale=-1.0)
+        for h in range(2):
+            nc.vector.tensor_tensor(f3[:].indirect(half(idx5, h)), at4[h][:], minus_at3[h][:], ALU.add)
+
+        aa = sb.tile([P, T], F32, name="aa")
+        nc.vector.tensor_tensor(aa[:], a[:], f3[:], ALU.add)
+
+        y = [sb.tile([P, HALF], F32, name=f"y{h}") for h in range(2)]
+        nc.scalar.activation(y[0][:], aa[:].indirect(half(idx, 0)), COPY)
+        nc.scalar.dma_start(out[:, 0:HALF], y[0][:])
+        nc.vector.tensor_copy(y[1][:], aa[:].indirect(half(idx, 1)))
+        nc.sync.dma_start(out[:, HALF:I], y[1][:])

@@ -77,37 +77,38 @@ def tile_attend_meetinghall_two_kernel(tc, query, keys_words, keys_scales, notes
         nc.vector.memset(f3[:].bitcast(I32), 0)
 
         a = sb.tile([P, T], F32, name="a")
-        for piece in range(4):
-            cols = slice(piece * 256, (piece + 1) * 256)
+        start = 0
+        for piece, width in enumerate((256, 256, 256, 128, 128)):
+            cols = slice(start, start + width)
+            start = cols.stop
             bank = ps.tile([P, 512], F32, name=f"a_bank{piece}", tag=f"bank{piece}")
             nc.tensor.matmul_mx(
-                out=bank[:, 0:256],
+                out=bank[:, 0:width],
                 lhsT=q_codes[:].bitcast(FP8X4), lhsT_scale=q_plane[:],
                 rhs=key_words[:, 2 * cols.start : 2 * cols.stop].bitcast(FP4X4), rhs_scale=key_plane[:, cols],
                 start=True, stop=True,
             )
-            if piece % 2 == 0:
-                nc.scalar.activation(a[:, cols], bank[:, 0:256], COPY)
+            if piece in (0, 2):
+                nc.scalar.activation(a[:, cols], bank[:, 0:width], COPY)
             else:
-                nc.vector.tensor_copy(a[:, cols], bank[:, 0:256])
+                nc.vector.tensor_copy(a[:, cols], bank[:, 0:width])
 
-        a_picked = [sb.tile([P, HALF], F32, name=f"a_picked{h}") for h in range(2)]
-        nc.scalar.activation(a_picked[0][:], a[:].indirect(half(idx, 0)), COPY)
-        nc.vector.tensor_copy(a_picked[1][:], a[:].indirect(half(idx, 1)))
-        for h in range(2):
-            nc.vector.tensor_copy(f1[:].indirect(half(idx3, h)), a_picked[h][:])
+        a_picked = sb.tile([P, I], F32, name="a_picked")
+        nc.scalar.activation(a_picked[:, 0:HALF], a[:].indirect(half(idx, 0)), COPY)
+        nc.vector.tensor_copy(a_picked[:, HALF:I], a[:].indirect(half(idx, 1)))
+        nc.vector.tensor_copy(f1[:].indirect(idx3[:]), a_picked[:])
 
         b = sb.tile([P, T], F32, name="b")
-        for piece in range(2):
-            cols = slice(piece * 512, (piece + 1) * 512)
-            bank = ps.tile([P, 512], F32, name=f"b_bank{piece}", tag=f"bank{2 + piece}")
+        for piece, bank_no in enumerate((4, 3, 5, 6)):
+            cols = slice(piece * 256, (piece + 1) * 256)
+            bank = ps.tile([P, 512], F32, name=f"b_bank{piece}", tag=f"bank{bank_no}")
             nc.tensor.matmul_mx(
-                out=bank[:],
+                out=bank[:, 0:256],
                 lhsT=q_codes[:].bitcast(FP8X4), lhsT_scale=q_plane[:],
                 rhs=note_words[:, cols].bitcast(FP8X4), rhs_scale=note_plane[:, cols],
                 start=True, stop=True,
             )
-            nc.scalar.activation(b[:, cols], bank[:], COPY)
+            nc.scalar.activation(b[:, cols], bank[:, 0:256], COPY)
         b_picked = sb.tile([P, I], F32, name="b_picked")
         nc.scalar.activation(b_picked[:], b[:].indirect(idx2[:]), COPY)
         nc.vector.tensor_copy(f2[:].indirect(idx4[:]), b_picked[:])
@@ -117,8 +118,8 @@ def tile_attend_meetinghall_two_kernel(tc, query, keys_words, keys_scales, notes
 
         at4 = [sb.tile([P, HALF], F32, name=f"at4_{h}") for h in range(2)]
         minus_at3 = [sb.tile([P, HALF], F32, name=f"minus_at3_{h}") for h in range(2)]
-        nc.scalar.activation(at4[0][:], m1[:].indirect(half(idx4, 0)), COPY)
-        nc.vector.tensor_scalar(minus_at3[0][:], m1[:].indirect(half(idx3, 0)), -1.0, 0.0, ALU.mult, ALU.add)
+        nc.scalar.activation(minus_at3[0][:], m1[:].indirect(half(idx3, 0)), COPY, scale=-1.0)
+        nc.vector.tensor_copy(at4[0][:], m1[:].indirect(half(idx4, 0)))
         nc.scalar.activation(at4[1][:], m1[:].indirect(half(idx4, 1)), COPY)
         nc.scalar.activation(minus_at3[1][:], m1[:].indirect(half(idx3, 1)), COPY, scale=-1.0)
         for h in range(2):

@@ -77,6 +77,7 @@ def tile_attend_meetinghall_two_kernel(tc, query, keys_words, keys_scales, notes
         nc.vector.memset(f3[:].bitcast(I32), 0)
 
         a = sb.tile([P, T], F32, name="a")
+        a_banks = []
         start = 0
         for piece, width in enumerate((256, 256, 256, 128, 128)):
             cols = slice(start, start + width)
@@ -88,6 +89,7 @@ def tile_attend_meetinghall_two_kernel(tc, query, keys_words, keys_scales, notes
                 rhs=key_words[:, 2 * cols.start : 2 * cols.stop].bitcast(FP4X4), rhs_scale=key_plane[:, cols],
                 start=True, stop=True,
             )
+            a_banks.append(bank)
             if piece in (0, 2):
                 nc.scalar.activation(a[:, cols], bank[:, 0:width], COPY)
             else:
@@ -126,7 +128,10 @@ def tile_attend_meetinghall_two_kernel(tc, query, keys_words, keys_scales, notes
             nc.vector.tensor_tensor(f3[:].indirect(half(idx5, h)), at4[h][:], minus_at3[h][:], ALU.add)
 
         aa = sb.tile([P, T], F32, name="aa")
-        nc.vector.tensor_tensor(aa[:], a[:], f3[:], ALU.add)
+        nc.gpsimd.tensor_tensor(aa[:, 704:T], a[:, 704:T], f3[:, 704:T], ALU.add)
+        for piece, width in enumerate((256, 256, 192)):
+            cols = slice(256 * piece, 256 * piece + width)
+            nc.vector.tensor_tensor(aa[:, cols], a_banks[piece][:, 0:width], f3[:, cols], ALU.add)
 
         y = [sb.tile([P, HALF], F32, name=f"y{h}") for h in range(2)]
         nc.scalar.activation(y[0][:], aa[:].indirect(half(idx, 0)), COPY)

import concourse.mybir as mybir

F32 = mybir.dt.float32
BF16 = mybir.dt.bfloat16
I32 = mybir.dt.int32
U32 = mybir.dt.uint32
U16 = mybir.dt.uint16
U8 = mybir.dt.uint8
FP8X4 = mybir.dt.float8_e4m3fn_x4
FP4X4 = mybir.dt.float4_e2m1fn_x4
ALU = mybir.AluOpType
COPY = mybir.ActivationFunctionType.Copy

P = 128
PACK = 4
D, T, I, Q = 512, 1024, 512, 128
HALF = I // 2
LIST_COLS = I // 16
FLOPS = 2 * 2 * D * Q * T


def tile_attend_meetinghall_two_kernel(tc, query, keys_words, keys_scales, notes_words, notes_scales,
                                        offs, offs2, offs3, offs4, offs5, out):
    nc = tc.nc
    with (
        tc.tile_pool(name="lists", bufs=1) as lists,
        tc.tile_pool(name="sb", bufs=1) as sb,
        tc.psum_pool(name="ps", bufs=1) as ps,
    ):
        def load_list(name, src):
            tile = lists.tile([P, LIST_COLS], U16, name=name)
            nc.sync.dma_start(tile[:], src)
            return tile

        def half(tile, h):
            return tile[:, h * LIST_COLS // 2 : (h + 1) * LIST_COLS // 2]

        def load_scales(plane, src):
            rows = src[0].bitcast(I32)
            for quad in range(4):
                nc.sync.dma_start(plane[32 * quad : 32 * quad + 4, :].bitcast(I32), rows[4 * quad : 4 * quad + 4, :])

        key_plane = sb.tile([P, T], U8, name="key_plane", align_bytes=64)
        note_plane = sb.tile([P, T], U8, name="note_plane", align_bytes=64)
        nc.vector.memset(key_plane[:].bitcast(I32), 0)
        nc.vector.memset(note_plane[:].bitcast(I32), 0)

        q_raw = sb.tile([P, PACK, Q], F32, name="q_raw")
        nc.sync.dma_start(q_raw[:], query.rearrange("(p j) q -> p j q", j=PACK))
        key_words = sb.tile([P, 2 * T], U8, name="key_words", align_bytes=64)
        nc.sync.dma_start(key_words[:].bitcast(I32), keys_words[0].bitcast(I32))
        load_scales(key_plane, keys_scales)
        idx = load_list("idx", offs)
        idx3 = load_list("idx3", offs3)
        note_words = sb.tile([P, T], U32, name="note_words", align_bytes=64)
        nc.sync.dma_start(note_words[:].bitcast(I32), notes_words[0].rearrange("p n t -> p (n t)").bitcast(I32))
        load_scales(note_plane, notes_scales)
        idx2 = load_list("idx2", offs2)
        idx4 = load_list("idx4", offs4)
        idx5 = load_list("idx5", offs5)

        f1 = sb.tile([P, T], F32, name="f1")
        f2 = sb.tile([P, T], F32, name="f2")
        nc.vector.memset(f1[:].bitcast(I32), 0)
        nc.vector.memset(f2[:].bitcast(I32), 0)

        q_bf = sb.tile([P, Q * PACK], BF16, name="q_bf", tag="q_bf_then_f3", align_bytes=64)
        nc.vector.tensor_copy(
            q_bf[:].rearrange("p (c i t) -> p c t i", i=4, t=PACK),
            q_raw[:].rearrange("p t (c i) -> p c t i", i=4),
        )
        q_codes = sb.tile([P, Q], U32, name="q_codes", align_bytes=64)
        q_plane = sb.tile([P, Q], U8, name="q_plane", align_bytes=64)
        nc.vector.quantize_mx(out=q_codes[:].bitcast(FP8X4), scales=q_plane[:], in_=q_bf[:])

        f3 = sb.tile([P, T], F32, name="f3", tag="q_bf_then_f3", align_bytes=64)
        nc.vector.memset(f3[:].bitcast(I32), 0)

        a = sb.tile([P, T], F32, name="a")
        a_banks = []
        start = 0
        for piece, width in enumerate((256, 256, 256, 128, 128)):
            cols = slice(start, start + width)
            start = cols.stop
            bank = ps.tile([P, 512], F32, name=f"a_bank{piece}", tag=f"bank{piece}")
            nc.tensor.matmul_mx(
                out=bank[:, 0:width],
                lhsT=q_codes[:].bitcast(FP8X4), lhsT_scale=q_plane[:],
                rhs=key_words[:, 2 * cols.start : 2 * cols.stop].bitcast(FP4X4), rhs_scale=key_plane[:, cols],
                start=True, stop=True,
            )
            a_banks.append(bank)
            if piece in (0, 2):
                nc.scalar.activation(a[:, cols], bank[:, 0:width], COPY)
            else:
                nc.vector.tensor_copy(a[:, cols], bank[:, 0:width])

        a_picked = sb.tile([P, I], F32, name="a_picked")
        nc.scalar.activation(a_picked[:, 0:HALF], a[:].indirect(half(idx, 0)), COPY)
        nc.vector.tensor_copy(a_picked[:, HALF:I], a[:].indirect(half(idx, 1)))
        nc.vector.tensor_copy(f1[:].indirect(idx3[:]), a_picked[:])

        b = sb.tile([P, T], F32, name="b")
        for piece, bank_no in enumerate((4, 3, 5, 6)):
            cols = slice(piece * 256, (piece + 1) * 256)
            bank = ps.tile([P, 512], F32, name=f"b_bank{piece}", tag=f"bank{bank_no}")
            nc.tensor.matmul_mx(
                out=bank[:, 0:256],
                lhsT=q_codes[:].bitcast(FP8X4), lhsT_scale=q_plane[:],
                rhs=note_words[:, cols].bitcast(FP8X4), rhs_scale=note_plane[:, cols],
                start=True, stop=True,
            )
            nc.scalar.activation(b[:, cols], bank[:, 0:256], COPY)
        b_picked = sb.tile([P, I], F32, name="b_picked")
        nc.scalar.activation(b_picked[:], b[:].indirect(idx2[:]), COPY)
        nc.vector.tensor_copy(f2[:].indirect(idx4[:]), b_picked[:])

        m1 = sb.tile([P, T], F32, name="m1")
        nc.vector.tensor_tensor(m1[:], f1[:], f2[:], ALU.max)

        at4 = [sb.tile([P, HALF], F32, name=f"at4_{h}") for h in range(2)]
        minus_at3 = [sb.tile([P, HALF], F32, name=f"minus_at3_{h}") for h in range(2)]
        nc.scalar.activation(minus_at3[0][:], m1[:].indirect(half(idx3, 0)), COPY, scale=-1.0)
        nc.vector.tensor_copy(at4[0][:], m1[:].indirect(half(idx4, 0)))
        nc.scalar.activation(at4[1][:], m1[:].indirect(half(idx4, 1)), COPY)
        nc.scalar.activation(minus_at3[1][:], m1[:].indirect(half(idx3, 1)), COPY, scale=-1.0)
        for h in range(2):
            nc.vector.tensor_tensor(f3[:].indirect(half(idx5, h)), at4[h][:], minus_at3[h][:], ALU.add)

        aa = sb.tile([P, T], F32, name="aa")
        nc.gpsimd.tensor_tensor(aa[:, 704:T], a[:, 704:T], f3[:, 704:T], ALU.add)
        for piece, width in enumerate((256, 256, 192)):
            cols = slice(256 * piece, 256 * piece + width)
            nc.vector.tensor_tensor(aa[:, cols], a_banks[piece][:, 0:width], f3[:, cols], ALU.add)

        y = [sb.tile([P, HALF], F32, name=f"y{h}") for h in range(2)]
        nc.scalar.activation(y[0][:], aa[:].indirect(half(idx, 0)), COPY)
        nc.scalar.dma_start(out[:, 0:HALF], y[0][:])
        nc.vector.tensor_copy(y[1][:], aa[:].indirect(half(idx, 1)))
        nc.sync.dma_start(out[:, HALF:I], y[1][:])
